import numpy as np
import ml_dtypes


def mxq(x, axis, fmt="e4m3"):
    dtype, down = {"e4m3": (ml_dtypes.float8_e4m3fn, 7), "e5m2": (ml_dtypes.float8_e5m2, 14)}[fmt]
    v = np.moveaxis(np.asarray(x, np.float32).astype(ml_dtypes.bfloat16).astype(np.float64), axis, -1)
    blocks = v.reshape(v.shape[:-1] + (-1, 32))
    amax = np.abs(blocks).max(-1, keepdims=True)
    byte = np.maximum(np.where(amax > 0, np.frexp(amax)[1] - 1 + 127, 0) - down, 1)
    scale = np.exp2(byte - 127.0)
    codes = (blocks / scale).astype(np.float32).astype(dtype).astype(np.float64)
    return np.moveaxis((codes * scale).reshape(v.shape), -1, axis)


WIDE = False


def mx_kscale(k):
    if not WIDE:
        return np.ones(k)
    levels = np.array([10, -10, 5, -5, 0])
    if k % 512:
        return np.exp2(np.random.permutation(np.resize(levels, k // 32))).repeat(32)
    a = np.empty((k // 512, 16))
    for p in range(k // 512):
        a[p, :8] = np.random.permutation(np.resize(levels, 8))
        for g in range(8):
            far = levels[np.abs(levels - a[p, g]) >= 10]
            a[p, g + 8] = far[np.random.randint(len(far))]
    return np.exp2(a.ravel()).repeat(32)


def f64(x):
    return np.asarray(x).astype(np.float64)


def striped8(idx):
    return np.concatenate([v.reshape(-1, 16).T for v in idx]).astype(np.uint16)


def unstriped8(offs):
    return np.stack([offs[16 * g:16 * g + 16].T.reshape(-1) for g in range(8)]).astype(np.int64)


E2M1 = np.array([0.0, 0.5, 1.0, 1.5, 2.0, 3.0, 4.0, 6.0, -0.0, -0.5, -1.0, -1.5, -2.0, -3.0, -4.0, -6.0])


def pack_weight(w, fmt):
    k, n = w.shape
    w = f64(np.asarray(w, np.float32).astype(ml_dtypes.bfloat16)).reshape(k // 32, 32, n)
    amax = np.abs(w).max(1)
    if fmt == "e4m3":
        byte = np.frexp(amax)[1] - 1 + 127 - 7
    else:
        mant, ex = np.frexp(amax / 6.0)
        byte = np.where(mant > 0.5, ex, ex - 1) + 127
    byte = np.clip(np.where(amax > 0, byte, 1), 1, 254)
    scaled = (w * np.exp2(127.0 - byte)[:, None, :]).reshape(k, n).astype(np.float32)
    by_word = np.ascontiguousarray(scaled.reshape(k // 512, 128, 4, n).transpose(0, 1, 3, 2))
    if fmt == "e4m3":
        words = by_word.astype(ml_dtypes.float8_e4m3fn).view(np.uint8)
    else:
        c = by_word.astype(ml_dtypes.float4_e2m1fn).view(np.uint8) & 0xF
        words = (c[..., 0::2] | (c[..., 1::2] << 4)).reshape(k // 512, 128, 2 * n)
    return np.ascontiguousarray(words), np.ascontiguousarray(byte.astype(np.uint8).reshape(k // 512, 16, n))


def unpack_weight(words, scales, fmt):
    g, _, n = scales.shape
    words = np.ascontiguousarray(words).reshape(g, 128, n, -1)
    if fmt == "e4m3":
        vals = words.view(ml_dtypes.float8_e4m3fn).astype(np.float64)
    else:
        nib = np.empty((g, 128, n, 4), np.uint8)
        nib[..., 0::2] = words & 0xF
        nib[..., 1::2] = words >> 4
        vals = E2M1[nib]
    vals = vals * np.repeat(np.exp2(scales.astype(np.float64) - 127.0), 8, axis=1)[..., None]
    return vals.transpose(0, 1, 3, 2).reshape(g * 512, n)


K, M, T, S = 1024, 512, 1024, 512


def setup_inputs():
    n = np.random.standard_normal
    s = mx_kscale(K)[:, None]
    p_w = pack_weight(n((K, M)) / np.sqrt(K) / s, "e2m1")
    return {
        "xT": (n((K, T)) * s).astype(np.float32),
        "w_words": p_w[0],
        "w_scales": p_w[1],
        "wgt": np.repeat(np.random.uniform(0.5, 2.0, (8, S)), 16, axis=0).astype(np.float32),
        "b": (0.3 * n(512)).astype(np.float32),
        "wgo": np.repeat(np.random.uniform(0.5, 2.0, (8, S)), 16, axis=0).astype(np.float32),
        "offs": striped8(np.stack([np.random.permutation(T)[:S] for _ in range(8)])),
        "offs2": striped8(np.stack([np.random.permutation(T)[:S] for _ in range(8)])),
    }


def reference(xT, w_words, w_scales, wgt, b, wgo, offs, offs2):
    idx = unstriped8(offs)
    group = np.arange(K) % 512 // 64
    xg = f64(wgt)[np.arange(K) // 4 % 128] * f64(xT)[np.arange(K)[:, None], idx[group]]
    xT_ = mxq(xg, 0, "e4m3")
    w_ = unpack_weight(w_words, w_scales, "e2m1")
    y = w_.T @ xT_
    place = unstriped8(offs2)[np.arange(M) % 128 // 16]
    out = np.zeros((M, T))
    out[np.arange(M)[:, None], place] = f64(wgo)[np.arange(M) % 128] * (y + f64(b)[:, None])
    return out

@@ -1,0 +1,163 @@
+from contextlib import ExitStack
+
+import concourse.mybir as mybir
+from concourse.masks import make_identity
+
+K, M, T, S = 1024, 512, 1024, 512
+FLOPS = 2 * K * M * S
+
+F32 = mybir.dt.float32
+BF16 = mybir.dt.bfloat16
+U32 = mybir.dt.uint32
+I32 = mybir.dt.int32
+U16 = mybir.dt.uint16
+U8 = mybir.dt.uint8
+FP8X4 = mybir.dt.float8_e4m3fn_x4
+FP4X4 = mybir.dt.float4_e2m1fn_x4
+MULT = mybir.AluOpType.mult
+IDENT = mybir.ActivationFunctionType.Identity
+
+P = 128
+H = 256
+SUB = 128
+M_TILES = M // P
+
+
+def tile_list_hboth_bias_kernel(tc, xT, w_words, w_scales, wgt, b, wgo, offs, offs2, out):
+    nc = tc.nc
+    with ExitStack() as ctx:
+        hold = ctx.enter_context(tc.tile_pool(name="hold", bufs=1))
+        psum = ctx.enter_context(tc.psum_pool(name="psum", bufs=1))
+
+        offs_sb = hold.tile([P, S // 16], U16, name="offs_sb")
+        offs2_sb = hold.tile([P, S // 16], U16, name="offs2_sb")
+        wgt_sb = [hold.tile([P, H], F32, name=f"wgt{h}") for h in range(2)]
+        wgo_sb = hold.tile([P, S], F32, name="wgo_sb")
+        planes = [hold.tile([P, T], F32, name=f"plane{k}") for k in range(8)]
+        w_sb = hold.tile([P, 2 * 2 * M], U8, name="w_sb", align_bytes=64)
+        ws_sb = hold.tile([P, 2 * M], U8, name="ws_sb", align_bytes=64)
+        b_rows = hold.tile([P, P], F32, name="b_rows")
+        ident = hold.tile([P, P], F32, name="ident")
+        bias = hold.tile([P, M_TILES], F32, name="bias")
+        picked = [[hold.tile([P, 4, H], F32, name=f"picked{a}{h}") for h in range(2)] for a in range(2)]
+        grouped = [[hold.tile([P, H, 4], BF16, name=f"grouped{a}{h}", align_bytes=64) for h in range(2)] for a in range(2)]
+        codes = [[hold.tile([P, H], U32, name=f"codes{a}{h}", align_bytes=64) for h in range(2)] for a in range(2)]
+        scales = [[hold.tile([P, H], U8, name=f"scales{a}{h}", align_bytes=64) for h in range(2)] for a in range(2)]
+        y_sb = [[hold.tile([P, H], F32, name=f"y{m}{h}") for h in range(2)] for m in range(M_TILES)]
+        windows = [hold.tile([P, T], F32, name=f"window{m}") for m in range(M_TILES)]
+
+        x_view = xT.rearrange("(a p i) t -> a i p t", p=P, i=4)
+
+        def load_plane(k):
+            nc.sync.dma_start(out=planes[k][:], in_=x_view[k // 4, k % 4])
+
+        nc.vector.memset(ws_sb[:].bitcast(I32), 0)
+        nc.gpsimd.memset(b_rows[:], 0.0)
+        nc.sync.dma_start(out=offs_sb[:], in_=offs)
+        nc.sync.dma_start(out=wgt_sb[0][:], in_=wgt[:, 0:H])
+        load_plane(0)
+        nc.sync.dma_start(out=wgt_sb[1][:], in_=wgt[:, H:S])
+        for k in range(1, 4):
+            load_plane(k)
+        ws_rows = ws_sb[:].bitcast(I32).rearrange("p (a n) -> p a n", a=2)
+        ws_hbm = w_scales.bitcast(I32).rearrange("a q n -> q a n")
+        for quad in range(4):
+            nc.sync.dma_start(out=ws_rows[32 * quad : 32 * quad + 4], in_=ws_hbm[4 * quad : 4 * quad + 4])
+        nc.sync.dma_start(out=b_rows[0:M_TILES, :], in_=b.rearrange("(m p) -> m p", p=P))
+        for k in range(4, 8):
+            load_plane(k)
+        nc.sync.dma_start(
+            out=w_sb[:].bitcast(I32).rearrange("p (a n) -> p a n", a=2),
+            in_=w_words.bitcast(I32).rearrange("a p n -> p a n"),
+        )
+        nc.sync.dma_start(out=offs2_sb[:], in_=offs2)
+        nc.sync.dma_start(out=wgo_sb[:], in_=wgo)
+
+        for m in range(M_TILES):
+            nc.vector.memset(windows[m][:], 0.0)
+
+        make_identity(nc, ident[:])
+        b_t = psum.tile([P, P], F32, name="b_t", tag="bank7")
+        nc.tensor.transpose(b_t[:], b_rows[:], ident[:])
+        nc.scalar.copy(out=bias[:], in_=b_t[:, 0:M_TILES])
+
+        banks = [[psum.tile([P, H], F32, name=f"acc{m}{h}", tag=f"bank{4 * h + m}") for h in range(2)] for m in range(M_TILES)]
+
+        def gather(k, h):
+            cols = slice(h * H // 16, (h + 1) * H // 16)
+            nc.vector.tensor_tensor(
+                picked[k // 4][h][:, k % 4, :], planes[k][:].indirect(offs_sb[:, cols]), wgt_sb[h][:], MULT
+            )
+
+        def cast(a, h):
+            nc.scalar.copy(out=grouped[a][h][:], in_=picked[a][h][:].rearrange("p i n -> p n i"))
+
+        def quantize(a, h):
+            nc.vector.quantize_mx(
+                out=codes[a][h][:].bitcast(FP8X4),
+                scales=scales[a][h][:],
+                in_=grouped[a][h][:].rearrange("p n i -> p (n i)"),
+            )
+
+        def multiply(m, h):
+            for s in range(H // SUB):
+                cols = slice(s * SUB, (s + 1) * SUB)
+                for a in range(2):
+                    nc.tensor.matmul_mx(
+                        out=banks[m][h][:, cols],
+                        lhsT=w_sb[:, 2 * (a * M + m * P) : 2 * (a * M + (m + 1) * P)].bitcast(FP4X4),
+                        lhsT_scale=ws_sb[:, a * M + m * P : a * M + (m + 1) * P],
+                        rhs=codes[a][h][:, cols].bitcast(FP8X4),
+                        rhs_scale=scales[a][h][:, cols],
+                        start=(a == 0),
+                        stop=(a == 1),
+                    )
+
+        def drain(m, h):
+            nc.scalar.activation(out=y_sb[m][h][:], in_=banks[m][h][:], func=IDENT, bias=bias[:, m : m + 1])
+
+        def scatter(m, h):
+            cols = slice(h * H // 16, (h + 1) * H // 16)
+            nc.vector.tensor_tensor(
+                windows[m][:].indirect(offs2_sb[:, cols]), y_sb[m][h][:], wgo_sb[:, h * H : (h + 1) * H], MULT
+            )
+
+        def store(m):
+            nc.sync.dma_start(out=out[m * P : (m + 1) * P, :], in_=windows[m][:])
+
+        for k in range(4):
+            gather(k, 0)
+            if k == 3:
+                cast(0, 0)
+            gather(k, 1)
+        cast(0, 1)
+        gather(4, 0)
+        gather(5, 0)
+        quantize(0, 0)
+        gather(6, 0)
+        gather(4, 1)
+        quantize(0, 1)
+        gather(7, 0)
+        cast(1, 0)
+        gather(5, 1)
+        gather(6, 1)
+        quantize(1, 0)
+        gather(7, 1)
+        for m in range(M_TILES):
+            multiply(m, 0)
+        drain(0, 0)
+        drain(1, 0)
+        cast(1, 1)
+        drain(2, 0)
+        drain(3, 0)
+        scatter(0, 0)
+        scatter(1, 0)
+        quantize(1, 1)
+        for m in range(M_TILES):
+            multiply(m, 1)
+            drain(m, 1)
+        scatter(2, 0)
+        scatter(3, 0)
+        for m in range(M_TILES):
+            scatter(m, 1)
+            store(m)

@@ -40,9 +40,9 @@ def tile_list_hboth_bias_kernel(tc, xT, w_words, w_scales, wgt, b, wgo, offs, of
         ident = hold.tile([P, P], F32, name="ident")
         bias = hold.tile([P, M_TILES], F32, name="bias")
         picked = [[hold.tile([P, 4, H], F32, name=f"picked{a}{h}") for h in range(2)] for a in range(2)]
-        grouped = [[hold.tile([P, H, 4], BF16, name=f"grouped{a}{h}", align_bytes=64) for h in range(2)] for a in range(2)]
-        codes = [[hold.tile([P, H], U32, name=f"codes{a}{h}", align_bytes=64) for h in range(2)] for a in range(2)]
-        scales = [[hold.tile([P, H], U8, name=f"scales{a}{h}", align_bytes=64) for h in range(2)] for a in range(2)]
+        grouped = [hold.tile([P, 2 * H, 4], BF16, name=f"grouped{h}", align_bytes=64) for h in range(2)]
+        codes = [hold.tile([P, 2 * H], U32, name=f"codes{h}", align_bytes=64) for h in range(2)]
+        scales = [hold.tile([P, 2 * H], U8, name=f"scales{h}", align_bytes=64) for h in range(2)]
         y_sb = [[hold.tile([P, H], F32, name=f"y{m}{h}") for h in range(2)] for m in range(M_TILES)]
         windows = [hold.tile([P, T], F32, name=f"window{m}") for m in range(M_TILES)]
 
@@ -54,7 +54,7 @@ def tile_list_hboth_bias_kernel(tc, xT, w_words, w_scales, wgt, b, wgo, offs, of
         nc.vector.memset(ws_sb[:].bitcast(I32), 0)
         nc.gpsimd.memset(b_rows[:], 0.0)
         nc.sync.dma_start(out=offs_sb[:], in_=offs)
-        nc.sync.dma_start(out=wgt_sb[0][:], in_=wgt[:, 0:H])
+        nc.scalar.dma_start(out=wgt_sb[0][:], in_=wgt[:, 0:H])
         load_plane(0)
         nc.sync.dma_start(out=wgt_sb[1][:], in_=wgt[:, H:S])
         for k in range(1, 4):
@@ -90,13 +90,13 @@ def tile_list_hboth_bias_kernel(tc, xT, w_words, w_scales, wgt, b, wgo, offs, of
             )
 
         def cast(a, h):
-            nc.scalar.copy(out=grouped[a][h][:], in_=picked[a][h][:].rearrange("p i n -> p n i"))
+            nc.scalar.copy(out=grouped[h][:, a * H : (a + 1) * H, :], in_=picked[a][h][:].rearrange("p i n -> p n i"))
 
-        def quantize(a, h):
+        def quantize(h):
             nc.vector.quantize_mx(
-                out=codes[a][h][:].bitcast(FP8X4),
-                scales=scales[a][h][:],
-                in_=grouped[a][h][:].rearrange("p n i -> p (n i)"),
+                out=codes[h][:].bitcast(FP8X4),
+                scales=scales[h][:],
+                in_=grouped[h][:].rearrange("p n i -> p (n i)"),
             )
 
         def multiply(m, h):
@@ -107,8 +107,8 @@ def tile_list_hboth_bias_kernel(tc, xT, w_words, w_scales, wgt, b, wgo, offs, of
                         out=banks[m][h][:, cols],
                         lhsT=w_sb[:, 2 * (a * M + m * P) : 2 * (a * M + (m + 1) * P)].bitcast(FP4X4),
                         lhsT_scale=ws_sb[:, a * M + m * P : a * M + (m + 1) * P],
-                        rhs=codes[a][h][:, cols].bitcast(FP8X4),
-                        rhs_scale=scales[a][h][:, cols],
+                        rhs=codes[h][:, a * H + s * SUB : a * H + (s + 1) * SUB].bitcast(FP8X4),
+                        rhs_scale=scales[h][:, a * H + s * SUB : a * H + (s + 1) * SUB],
                         start=(a == 0),
                         stop=(a == 1),
                     )
@@ -125,23 +125,17 @@ def tile_list_hboth_bias_kernel(tc, xT, w_words, w_scales, wgt, b, wgo, offs, of
         def store(m):
             nc.sync.dma_start(out=out[m * P : (m + 1) * P, :], in_=windows[m][:])
 
-        for k in range(4):
-            gather(k, 0)
-            if k == 3:
-                cast(0, 0)
-            gather(k, 1)
+        for k, h in ((0, 0), (0, 1), (1, 0), (1, 1), (2, 0), (2, 1), (3, 0)):
+            gather(k, h)
+        cast(0, 0)
+        for k, h in ((4, 0), (5, 0), (3, 1), (6, 0)):
+            gather(k, h)
         cast(0, 1)
-        gather(4, 0)
-        gather(5, 0)
-        quantize(0, 0)
-        gather(6, 0)
-        gather(4, 1)
-        quantize(0, 1)
         gather(7, 0)
         cast(1, 0)
-        gather(5, 1)
-        gather(6, 1)
-        quantize(1, 0)
+        for k in (4, 5, 6):
+            gather(k, 1)
+        quantize(0)
         gather(7, 1)
         for m in range(M_TILES):
             multiply(m, 0)
@@ -152,11 +146,11 @@ def tile_list_hboth_bias_kernel(tc, xT, w_words, w_scales, wgt, b, wgo, offs, of
         drain(3, 0)
         scatter(0, 0)
         scatter(1, 0)
-        quantize(1, 1)
+        scatter(2, 0)
+        quantize(1)
         for m in range(M_TILES):
             multiply(m, 1)
             drain(m, 1)
-        scatter(2, 0)
         scatter(3, 0)
         for m in range(M_TILES):
             scatter(m, 1)

@@ -53,9 +53,9 @@ def tile_list_hboth_bias_kernel(tc, xT, w_words, w_scales, wgt, b, wgo, offs, of
 
         nc.vector.memset(ws_sb[:].bitcast(I32), 0)
         nc.gpsimd.memset(b_rows[:], 0.0)
-        nc.sync.dma_start(out=offs_sb[:], in_=offs)
         nc.scalar.dma_start(out=wgt_sb[0][:], in_=wgt[:, 0:H])
         load_plane(0)
+        nc.sync.dma_start(out=offs_sb[:], in_=offs)
         nc.sync.dma_start(out=wgt_sb[1][:], in_=wgt[:, H:S])
         for k in range(1, 4):
             load_plane(k)
@@ -123,7 +123,12 @@ def tile_list_hboth_bias_kernel(tc, xT, w_words, w_scales, wgt, b, wgo, offs, of
             )
 
         def store(m):
-            nc.sync.dma_start(out=out[m * P : (m + 1) * P, :], in_=windows[m][:])
+            rows = slice(m * P, (m + 1) * P)
+            if m < M_TILES - 1:
+                nc.sync.dma_start(out=out[rows, :], in_=windows[m][:])
+            else:
+                nc.sync.dma_start(out=out[rows, 0 : T // 2], in_=windows[m][:, 0 : T // 2])
+                nc.scalar.dma_start(out=out[rows, T // 2 : T], in_=windows[m][:, T // 2 : T])
 
         for k, h in ((0, 0), (0, 1), (1, 0), (1, 1), (2, 0), (2, 1), (3, 0)):
             gather(k, h)
@@ -133,9 +138,10 @@ def tile_list_hboth_bias_kernel(tc, xT, w_words, w_scales, wgt, b, wgo, offs, of
         cast(0, 1)
         gather(7, 0)
         cast(1, 0)
-        for k in (4, 5, 6):
-            gather(k, 1)
+        gather(4, 1)
+        gather(5, 1)
         quantize(0)
+        gather(6, 1)
         gather(7, 1)
         for m in range(M_TILES):
             multiply(m, 0)

from contextlib import ExitStack

import concourse.mybir as mybir
from concourse.masks import make_identity

K, M, T, S = 1024, 512, 1024, 512
FLOPS = 2 * K * M * S

F32 = mybir.dt.float32
BF16 = mybir.dt.bfloat16
U32 = mybir.dt.uint32
I32 = mybir.dt.int32
U16 = mybir.dt.uint16
U8 = mybir.dt.uint8
FP8X4 = mybir.dt.float8_e4m3fn_x4
FP4X4 = mybir.dt.float4_e2m1fn_x4
MULT = mybir.AluOpType.mult
IDENT = mybir.ActivationFunctionType.Identity

P = 128
H = 256
SUB = 128
M_TILES = M // P


def tile_list_hboth_bias_kernel(tc, xT, w_words, w_scales, wgt, b, wgo, offs, offs2, out):
    nc = tc.nc
    with ExitStack() as ctx:
        hold = ctx.enter_context(tc.tile_pool(name="hold", bufs=1))
        psum = ctx.enter_context(tc.psum_pool(name="psum", bufs=1))

        offs_sb = hold.tile([P, S // 16], U16, name="offs_sb")
        offs2_sb = hold.tile([P, S // 16], U16, name="offs2_sb")
        wgt_sb = [hold.tile([P, H], F32, name=f"wgt{h}") for h in range(2)]
        wgo_sb = hold.tile([P, S], F32, name="wgo_sb")
        planes = [hold.tile([P, T], F32, name=f"plane{k}") for k in range(8)]
        w_sb = hold.tile([P, 2 * 2 * M], U8, name="w_sb", align_bytes=64)
        ws_sb = hold.tile([P, 2 * M], U8, name="ws_sb", align_bytes=64)
        b_rows = hold.tile([P, P], F32, name="b_rows")
        ident = hold.tile([P, P], F32, name="ident")
        bias = hold.tile([P, M_TILES], F32, name="bias")
        picked = [[hold.tile([P, 4, H], F32, name=f"picked{a}{h}") for h in range(2)] for a in range(2)]
        grouped = [hold.tile([P, 2 * H, 4], BF16, name=f"grouped{h}", align_bytes=64) for h in range(2)]
        codes = [hold.tile([P, 2 * H], U32, name=f"codes{h}", align_bytes=64) for h in range(2)]
        scales = [hold.tile([P, 2 * H], U8, name=f"scales{h}", align_bytes=64) for h in range(2)]
        y_sb = [[hold.tile([P, H], F32, name=f"y{m}{h}") for h in range(2)] for m in range(M_TILES)]
        windows = [hold.tile([P, T], F32, name=f"window{m}") for m in range(M_TILES)]

        x_view = xT.rearrange("(a p i) t -> a i p t", p=P, i=4)

        def load_plane(k):
            nc.sync.dma_start(out=planes[k][:], in_=x_view[k // 4, k % 4])

        nc.vector.memset(ws_sb[:].bitcast(I32), 0)
        nc.gpsimd.memset(b_rows[:], 0.0)
        nc.scalar.dma_start(out=wgt_sb[0][:], in_=wgt[:, 0:H])
        load_plane(0)
        nc.sync.dma_start(out=offs_sb[:], in_=offs)
        nc.sync.dma_start(out=wgt_sb[1][:], in_=wgt[:, H:S])
        for k in range(1, 4):
            load_plane(k)
        ws_rows = ws_sb[:].bitcast(I32).rearrange("p (a n) -> p a n", a=2)
        ws_hbm = w_scales.bitcast(I32).rearrange("a q n -> q a n")
        for quad in range(4):
            nc.sync.dma_start(out=ws_rows[32 * quad : 32 * quad + 4], in_=ws_hbm[4 * quad : 4 * quad + 4])
        nc.sync.dma_start(out=b_rows[0:M_TILES, :], in_=b.rearrange("(m p) -> m p", p=P))
        for k in range(4, 8):
            load_plane(k)
        nc.sync.dma_start(
            out=w_sb[:].bitcast(I32).rearrange("p (a n) -> p a n", a=2),
            in_=w_words.bitcast(I32).rearrange("a p n -> p a n"),
        )
        nc.sync.dma_start(out=offs2_sb[:], in_=offs2)
        nc.sync.dma_start(out=wgo_sb[:], in_=wgo)

        for m in range(M_TILES):
            nc.vector.memset(windows[m][:], 0.0)

        make_identity(nc, ident[:])
        b_t = psum.tile([P, P], F32, name="b_t", tag="bank7")
        nc.tensor.transpose(b_t[:], b_rows[:], ident[:])
        nc.scalar.copy(out=bias[:], in_=b_t[:, 0:M_TILES])

        banks = [[psum.tile([P, H], F32, name=f"acc{m}{h}", tag=f"bank{4 * h + m}") for h in range(2)] for m in range(M_TILES)]

        def gather(k, h):
            cols = slice(h * H // 16, (h + 1) * H // 16)
            nc.vector.tensor_tensor(
                picked[k // 4][h][:, k % 4, :], planes[k][:].indirect(offs_sb[:, cols]), wgt_sb[h][:], MULT
            )

        def cast(a, h):
            nc.scalar.copy(out=grouped[h][:, a * H : (a + 1) * H, :], in_=picked[a][h][:].rearrange("p i n -> p n i"))

        def quantize(h):
            nc.vector.quantize_mx(
                out=codes[h][:].bitcast(FP8X4),
                scales=scales[h][:],
                in_=grouped[h][:].rearrange("p n i -> p (n i)"),
            )

        def multiply(m, h):
            for s in range(H // SUB):
                cols = slice(s * SUB, (s + 1) * SUB)
                for a in range(2):
                    nc.tensor.matmul_mx(
                        out=banks[m][h][:, cols],
                        lhsT=w_sb[:, 2 * (a * M + m * P) : 2 * (a * M + (m + 1) * P)].bitcast(FP4X4),
                        lhsT_scale=ws_sb[:, a * M + m * P : a * M + (m + 1) * P],
                        rhs=codes[h][:, a * H + s * SUB : a * H + (s + 1) * SUB].bitcast(FP8X4),
                        rhs_scale=scales[h][:, a * H + s * SUB : a * H + (s + 1) * SUB],
                        start=(a == 0),
                        stop=(a == 1),
                    )

        def drain(m, h):
            nc.scalar.activation(out=y_sb[m][h][:], in_=banks[m][h][:], func=IDENT, bias=bias[:, m : m + 1])

        def scatter(m, h):
            cols = slice(h * H // 16, (h + 1) * H // 16)
            nc.vector.tensor_tensor(
                windows[m][:].indirect(offs2_sb[:, cols]), y_sb[m][h][:], wgo_sb[:, h * H : (h + 1) * H], MULT
            )

        def store(m):
            rows = slice(m * P, (m + 1) * P)
            if m < M_TILES - 1:
                nc.sync.dma_start(out=out[rows, :], in_=windows[m][:])
            else:
                nc.sync.dma_start(out=out[rows, 0 : T // 2], in_=windows[m][:, 0 : T // 2])
                nc.scalar.dma_start(out=out[rows, T // 2 : T], in_=windows[m][:, T // 2 : T])

        for k, h in ((0, 0), (0, 1), (1, 0), (1, 1), (2, 0), (2, 1), (3, 0)):
            gather(k, h)
        cast(0, 0)
        for k, h in ((4, 0), (5, 0), (3, 1), (6, 0)):
            gather(k, h)
        cast(0, 1)
        gather(7, 0)
        cast(1, 0)
        gather(4, 1)
        gather(5, 1)
        quantize(0)
        gather(6, 1)
        gather(7, 1)
        for m in range(M_TILES):
            multiply(m, 0)
        drain(0, 0)
        drain(1, 0)
        cast(1, 1)
        drain(2, 0)
        drain(3, 0)
        scatter(0, 0)
        scatter(1, 0)
        scatter(2, 0)
        quantize(1)
        for m in range(M_TILES):
            multiply(m, 1)
            drain(m, 1)
        scatter(3, 0)
        for m in range(M_TILES):
            scatter(m, 1)
            store(m)
